import numpy as np
import ml_dtypes

BF16 = ml_dtypes.bfloat16


def bf(x):
    return np.asarray(x, np.float32).astype(BF16)


def f32(x):
    return np.asarray(x, np.float32)


def f64(x):
    return np.asarray(x).astype(np.float64)


def striped(idx):
    return np.tile(idx.reshape(-1, 16).T, (8, 1))


S, K, M, N, E, Q, H = 512, 128, 256, 512, 8, 64, 128


def sigmoid(v):
    return 1.0 / (1.0 + np.exp(-v))


def setup_inputs():
    return {"table": bf(np.random.standard_normal((K, S))), "w": bf(np.random.standard_normal((E, K, M)) / np.sqrt(K)), "offs": striped(np.sort(np.random.permutation(S).reshape(E, Q), axis=1).reshape(-1))}


def reference(table, w, offs):
    idx = offs[:16].T.reshape(-1)
    x = f64(table)[:, idx]
    y = np.concatenate([f64(w)[e].T @ x[:, e * Q : (e + 1) * Q] for e in range(E)], axis=1)
    return y[:H] * sigmoid(y[H:])

@@ -1,0 +1,67 @@
+import concourse.mybir as mybir
+
+BF16, F32, U16 = mybir.dt.bfloat16, mybir.dt.float32, mybir.dt.uint16
+SIGMOID = mybir.ActivationFunctionType.Sigmoid
+MULT = mybir.AluOpType.mult
+
+P = 128
+S = 512
+N = 512
+E = 8
+Q = N // E
+QCOLS = Q // 16
+H = 128
+
+CHUNKS = 4
+EC = E // CHUNKS
+C = EC * Q
+BANK = 512
+WARM = 4
+
+FLOPS = 2 * P * 2 * H * N
+
+
+def tile_gather_matmul_kernel(tc, table, w, offs, out):
+    nc = tc.nc
+    with (
+        tc.tile_pool(name="held", bufs=1) as held,
+        tc.tile_pool(name="chunked", bufs=CHUNKS) as chunked,
+        tc.psum_pool(name="idle", bufs=1) as idle,
+        tc.psum_pool(name="psum", bufs=3) as psum,
+    ):
+        offsets = held.tile([P, N // 16], U16, name="offsets")
+        nc.sync.dma_start(offsets[:], offs)
+        tokens = held.tile([P, S], BF16, name="tokens")
+        nc.sync.dma_start(tokens[:], table)
+
+        weights = []
+        for c in range(CHUNKS):
+            chunk_weights = chunked.tile([P, EC, 2 * H], BF16, name="chunk_weights")
+            queue = nc.scalar if c % 2 == 0 else nc.sync
+            queue.dma_start(chunk_weights[:], w[c * EC : (c + 1) * EC].rearrange("e k m -> k e m"))
+            weights.append(chunk_weights)
+
+        zeros = held.tile([P, P], BF16, name="zeros")
+        nc.vector.memset(zeros[:], 0.0)
+        unread = idle.tile([P, BANK], F32, name="unread")
+        for _ in range(WARM):
+            nc.tensor.matmul(unread[:], zeros[:], zeros[:, 0:1].to_broadcast([P, BANK]), start=True, stop=True)
+
+        for c in range(CHUNKS):
+            gates = psum.tile([P, C], F32, name="gates")
+            values = psum.tile([P, C], F32, name="values")
+            for bank, first in ((gates, H), (values, 0)):
+                for i in range(EC):
+                    e = c * EC + i
+                    nc.tensor.matmul(
+                        bank[:, i * Q : (i + 1) * Q],
+                        weights[c][:, i, first : first + H],
+                        tokens[:].indirect(offsets[:, e * QCOLS : (e + 1) * QCOLS]),
+                        start=True,
+                        stop=True,
+                    )
+            opened = chunked.tile([P, C], F32, name="opened")
+            nc.scalar.activation(opened[:], gates[:], SIGMOID)
+            result = chunked.tile([P, C], F32, name="result")
+            nc.vector.tensor_tensor(result[:], values[:], opened[:], MULT)
+            nc.sync.dma_start(out[:, c * C : (c + 1) * C], result[:])

@@ -37,8 +37,12 @@ def tile_gather_matmul_kernel(tc, table, w, offs, out):
         weights = []
         for c in range(CHUNKS):
             chunk_weights = chunked.tile([P, EC, 2 * H], BF16, name="chunk_weights")
-            queue = nc.scalar if c % 2 == 0 else nc.sync
-            queue.dma_start(chunk_weights[:], w[c * EC : (c + 1) * EC].rearrange("e k m -> k e m"))
+            if c == 1:
+                for i, queue in enumerate((nc.scalar, nc.sync)):
+                    queue.dma_start(chunk_weights[:, i, :], w[c * EC + i])
+            else:
+                queue = nc.scalar if c % 2 == 0 else nc.sync
+                queue.dma_start(chunk_weights[:], w[c * EC : (c + 1) * EC].rearrange("e k m -> k e m"))
             weights.append(chunk_weights)
 
         zeros = held.tile([P, P], BF16, name="zeros")

@@ -37,11 +37,11 @@ def tile_gather_matmul_kernel(tc, table, w, offs, out):
         weights = []
         for c in range(CHUNKS):
             chunk_weights = chunked.tile([P, EC, 2 * H], BF16, name="chunk_weights")
-            if c == 1:
+            if 0 < c < CHUNKS - 1:
                 for i, queue in enumerate((nc.scalar, nc.sync)):
                     queue.dma_start(chunk_weights[:, i, :], w[c * EC + i])
             else:
-                queue = nc.scalar if c % 2 == 0 else nc.sync
+                queue = nc.scalar if c == 0 else nc.sync
                 queue.dma_start(chunk_weights[:], w[c * EC : (c + 1) * EC].rearrange("e k m -> k e m"))
             weights.append(chunk_weights)
 

@@ -37,12 +37,11 @@ def tile_gather_matmul_kernel(tc, table, w, offs, out):
         weights = []
         for c in range(CHUNKS):
             chunk_weights = chunked.tile([P, EC, 2 * H], BF16, name="chunk_weights")
-            if 0 < c < CHUNKS - 1:
+            if c == 0:
+                nc.scalar.dma_start(chunk_weights[:], w[0:EC].rearrange("e k m -> k e m"))
+            else:
                 for i, queue in enumerate((nc.scalar, nc.sync)):
                     queue.dma_start(chunk_weights[:, i, :], w[c * EC + i])
-            else:
-                queue = nc.scalar if c == 0 else nc.sync
-                queue.dma_start(chunk_weights[:], w[c * EC : (c + 1) * EC].rearrange("e k m -> k e m"))
             weights.append(chunk_weights)
 
         zeros = held.tile([P, P], BF16, name="zeros")

import concourse.mybir as mybir

BF16, F32, U16 = mybir.dt.bfloat16, mybir.dt.float32, mybir.dt.uint16
SIGMOID = mybir.ActivationFunctionType.Sigmoid
MULT = mybir.AluOpType.mult

P = 128
S = 512
N = 512
E = 8
Q = N // E
QCOLS = Q // 16
H = 128

CHUNKS = 4
EC = E // CHUNKS
C = EC * Q
BANK = 512
WARM = 4

FLOPS = 2 * P * 2 * H * N


def tile_gather_matmul_kernel(tc, table, w, offs, out):
    nc = tc.nc
    with (
        tc.tile_pool(name="held", bufs=1) as held,
        tc.tile_pool(name="chunked", bufs=CHUNKS) as chunked,
        tc.psum_pool(name="idle", bufs=1) as idle,
        tc.psum_pool(name="psum", bufs=3) as psum,
    ):
        offsets = held.tile([P, N // 16], U16, name="offsets")
        nc.sync.dma_start(offsets[:], offs)
        tokens = held.tile([P, S], BF16, name="tokens")
        nc.sync.dma_start(tokens[:], table)

        weights = []
        for c in range(CHUNKS):
            chunk_weights = chunked.tile([P, EC, 2 * H], BF16, name="chunk_weights")
            if c == 0:
                nc.scalar.dma_start(chunk_weights[:], w[0:EC].rearrange("e k m -> k e m"))
            else:
                for i, queue in enumerate((nc.scalar, nc.sync)):
                    queue.dma_start(chunk_weights[:, i, :], w[c * EC + i])
            weights.append(chunk_weights)

        zeros = held.tile([P, P], BF16, name="zeros")
        nc.vector.memset(zeros[:], 0.0)
        unread = idle.tile([P, BANK], F32, name="unread")
        for _ in range(WARM):
            nc.tensor.matmul(unread[:], zeros[:], zeros[:, 0:1].to_broadcast([P, BANK]), start=True, stop=True)

        for c in range(CHUNKS):
            gates = psum.tile([P, C], F32, name="gates")
            values = psum.tile([P, C], F32, name="values")
            for bank, first in ((gates, H), (values, 0)):
                for i in range(EC):
                    e = c * EC + i
                    nc.tensor.matmul(
                        bank[:, i * Q : (i + 1) * Q],
                        weights[c][:, i, first : first + H],
                        tokens[:].indirect(offsets[:, e * QCOLS : (e + 1) * QCOLS]),
                        start=True,
                        stop=True,
                    )
            opened = chunked.tile([P, C], F32, name="opened")
            nc.scalar.activation(opened[:], gates[:], SIGMOID)
            result = chunked.tile([P, C], F32, name="result")
            nc.vector.tensor_tensor(result[:], values[:], opened[:], MULT)
            nc.sync.dma_start(out[:, c * C : (c + 1) * C], result[:])
